import numpy as np, ml_dtypes
CORES = [1,2,9,10,17,18,25,26,33,34,41,42,49,50,57,58,65,66,73,74,81,82,89,90,97,98,105,106,113,114,121,122]
N = 32
H = 2
ROWS, COLS = 4, 8
PERIODIC = True
def setup_inputs(rng):
    return {"x": rng.standard_normal((N, 128, 512), dtype=np.float32).astype(ml_dtypes.bfloat16)}
def reference(x):
    W = x.shape[2]
    y = np.zeros((N, 4, 128, H), x.dtype)
    for r in range(N):
        i, j = divmod(r, COLS)
        for k, (di, dj, cols) in enumerate([(-1, 0, slice(W - H, W)), (1, 0, slice(0, H)), (0, -1, slice(W - H, W)), (0, 1, slice(0, H))]):
            a, b = i + di, j + dj
            if PERIODIC:
                a, b = a % ROWS, b % COLS
            if 0 <= a < ROWS and 0 <= b < COLS:
                y[r][k] = x[a * COLS + b][:, cols]
    return {"y": y}

@@ -1,0 +1,73 @@
+from concourse.bass import DstId, RemoteDMATransfer
+
+H = 2
+ROWS, COLS = 4, 8
+RELAY = 6
+
+SCRATCH = {
+    "edge": ("dram", [2, 128, H], "bfloat16"),
+    "halo": ("dram", [4, 128, H], "bfloat16"),
+    "hop": ("dram", [128, H], "bfloat16"),
+}
+SEMAPHORES = ["loaded", "sent", "arrived", "stored"]
+
+NORTH, SOUTH, WEST, EAST = 0, 1, 2, 3
+FIRST, LAST = 0, 1
+
+
+def _west_of(rank):
+    i, j = divmod(rank, COLS)
+    return i * COLS + (j - 1) % COLS
+
+
+def _dst(topo, core):
+    rid, pid, _se = topo.addr(core)
+    return DstId(rid=rid, pnc=pid)
+
+
+def rank_program(g, core, T, topo):
+    rank = T.rank_of(core)
+    sem = T.sem
+
+    if rank is None:
+        if core % 8 != RELAY:
+            return
+        client = T.rank_of(core - RELAY + 1)
+        if client is None or topo.may_write(T.cores[client], T.cores[_west_of(client)]):
+            return
+        to = T.cores[_west_of(client)]
+        rid, pid, _se = topo.addr(to)
+        g.wait_ge(sem.arrived, 1)
+        g.remote_dma(T.halo[EAST], T.hop[:], sem.arrived, sem.sent, pid, rid, 0x01)
+        g.wait_ge(sem.sent, 1)
+        return
+
+    i, j = divmod(rank, COLS)
+    W = T.x.shape[1]
+    north = T.cores[((i - 1) % ROWS) * COLS + j]
+    south = T.cores[((i + 1) % ROWS) * COLS + j]
+    west = T.cores[_west_of(rank)]
+    east = T.cores[i * COLS + (j + 1) % COLS]
+
+    g.sync.dma_start(T.edge[FIRST], T.x[:, 0:H]).then_inc(sem.loaded, 16)
+    g.scalar.dma_start(T.edge[LAST], T.x[:, W - H:W]).then_inc(sem.loaded, 16)
+    g.wait_ge(sem.loaded, 32)
+
+    if topo.may_write(core, west):
+        west_id, west_ap = _dst(topo, west), T.halo[EAST]
+    else:
+        west_id, west_ap = _dst(topo, core - core % 8 + RELAY), T.hop[:]
+    g.remote_dma_fused(
+        [
+            RemoteDMATransfer(dst_ids=[_dst(topo, north), west_id], dma_engine_mask=0x01, remote_sem=sem.arrived,
+                              srcs=[T.edge[FIRST]], dsts=[T.halo[SOUTH], west_ap]),
+            RemoteDMATransfer(dst_ids=[_dst(topo, south), _dst(topo, east)], dma_engine_mask=0x02,
+                              remote_sem=sem.arrived, srcs=[T.edge[LAST]], dsts=[T.halo[NORTH], T.halo[WEST]]),
+        ],
+        local_sem=sem.sent,
+    )
+
+    g.sync.wait_ge(sem.arrived, 4)
+    g.sync.dma_start(T.y[:], T.halo[:]).then_inc(sem.stored, 16)
+    g.wait_ge(sem.sent, 2)
+    g.wait_ge(sem.stored, 16)

@@ -7,7 +7,7 @@ RELAY = 6
 SCRATCH = {
     "edge": ("dram", [2, 128, H], "bfloat16"),
     "halo": ("dram", [4, 128, H], "bfloat16"),
-    "hop": ("dram", [128, H], "bfloat16"),
+    "hop": ("dram", [2, 128, H], "bfloat16"),
 }
 SEMAPHORES = ["loaded", "sent", "arrived", "stored"]
 
@@ -15,59 +15,63 @@ NORTH, SOUTH, WEST, EAST = 0, 1, 2, 3
 FIRST, LAST = 0, 1
 
 
-def _west_of(rank):
+def _neighbours(T, rank):
     i, j = divmod(rank, COLS)
-    return i * COLS + (j - 1) % COLS
+    return (T.cores[((i - 1) % ROWS) * COLS + j], T.cores[((i + 1) % ROWS) * COLS + j],
+            T.cores[i * COLS + (j - 1) % COLS], T.cores[i * COLS + (j + 1) % COLS])
 
 
-def _dst(topo, core):
-    rid, pid, _se = topo.addr(core)
-    return DstId(rid=rid, pnc=pid)
+def _send(g, T, topo, writes):
+    transfers = []
+    for k, (src, to, dst) in enumerate(writes):
+        rid, pid, _se = topo.addr(to)
+        transfers.append(RemoteDMATransfer(dst_ids=[DstId(rid=rid, pnc=pid)], dma_engine_mask=1 << k,
+                                           remote_sem=T.sem.arrived, src=src, dst=dst))
+    g.remote_dma_fused(transfers, local_sem=T.sem.sent)
+    return len(writes)
 
 
 def rank_program(g, core, T, topo):
     rank = T.rank_of(core)
     sem = T.sem
+    chip_base = core - core % 8
 
     if rank is None:
         if core % 8 != RELAY:
             return
-        client = T.rank_of(core - RELAY + 1)
-        if client is None or topo.may_write(T.cores[client], T.cores[_west_of(client)]):
-            return
-        to = T.cores[_west_of(client)]
-        rid, pid, _se = topo.addr(to)
-        g.wait_ge(sem.arrived, 1)
-        g.remote_dma(T.halo[EAST], T.hop[:], sem.arrived, sem.sent, pid, rid, 0x01)
-        g.wait_ge(sem.sent, 1)
+        north, south, west, _east = _neighbours(T, T.rank_of(chip_base + 1))
+        g.wait_ge(sem.arrived, 2)
+        n = _send(g, T, topo, [
+            (T.hop[FIRST], west, T.halo[EAST]),
+            (T.hop[FIRST], north, T.halo[SOUTH]),
+            (T.hop[LAST], south, T.halo[NORTH]),
+        ])
+        g.wait_ge(sem.sent, n)
         return
 
-    i, j = divmod(rank, COLS)
+    north, south, west, east = _neighbours(T, rank)
     W = T.x.shape[1]
-    north = T.cores[((i - 1) % ROWS) * COLS + j]
-    south = T.cores[((i + 1) % ROWS) * COLS + j]
-    west = T.cores[_west_of(rank)]
-    east = T.cores[i * COLS + (j + 1) % COLS]
 
     g.sync.dma_start(T.edge[FIRST], T.x[:, 0:H]).then_inc(sem.loaded, 16)
     g.scalar.dma_start(T.edge[LAST], T.x[:, W - H:W]).then_inc(sem.loaded, 16)
     g.wait_ge(sem.loaded, 32)
 
-    if topo.may_write(core, west):
-        west_id, west_ap = _dst(topo, west), T.halo[EAST]
+    if topo.may_write(core, west) and topo.may_write(core, east):
+        n = _send(g, T, topo, [
+            (T.edge[LAST], east, T.halo[WEST]),
+            (T.edge[FIRST], north, T.halo[SOUTH]),
+            (T.edge[LAST], south, T.halo[NORTH]),
+            (T.edge[FIRST], west, T.halo[EAST]),
+        ])
     else:
-        west_id, west_ap = _dst(topo, core - core % 8 + RELAY), T.hop[:]
-    g.remote_dma_fused(
-        [
-            RemoteDMATransfer(dst_ids=[_dst(topo, north), west_id], dma_engine_mask=0x01, remote_sem=sem.arrived,
-                              srcs=[T.edge[FIRST]], dsts=[T.halo[SOUTH], west_ap]),
-            RemoteDMATransfer(dst_ids=[_dst(topo, south), _dst(topo, east)], dma_engine_mask=0x02,
-                              remote_sem=sem.arrived, srcs=[T.edge[LAST]], dsts=[T.halo[NORTH], T.halo[WEST]]),
-        ],
-        local_sem=sem.sent,
-    )
+        relay = chip_base + RELAY
+        n = _send(g, T, topo, [
+            (T.edge[FIRST], relay, T.hop[FIRST]),
+            (T.edge[LAST], relay, T.hop[LAST]),
+            (T.edge[LAST], east, T.halo[WEST]),
+        ])
 
     g.sync.wait_ge(sem.arrived, 4)
     g.sync.dma_start(T.y[:], T.halo[:]).then_inc(sem.stored, 16)
-    g.wait_ge(sem.sent, 2)
+    g.wait_ge(sem.sent, n)
     g.wait_ge(sem.stored, 16)

from concourse.bass import DstId, RemoteDMATransfer

H = 2
ROWS, COLS = 4, 8
RELAY = 6

SCRATCH = {
    "edge": ("dram", [2, 128, H], "bfloat16"),
    "halo": ("dram", [4, 128, H], "bfloat16"),
    "hop": ("dram", [2, 128, H], "bfloat16"),
}
SEMAPHORES = ["loaded", "sent", "arrived", "stored"]

NORTH, SOUTH, WEST, EAST = 0, 1, 2, 3
FIRST, LAST = 0, 1


def _neighbours(T, rank):
    i, j = divmod(rank, COLS)
    return (T.cores[((i - 1) % ROWS) * COLS + j], T.cores[((i + 1) % ROWS) * COLS + j],
            T.cores[i * COLS + (j - 1) % COLS], T.cores[i * COLS + (j + 1) % COLS])


def _send(g, T, topo, writes):
    transfers = []
    for k, (src, to, dst) in enumerate(writes):
        rid, pid, _se = topo.addr(to)
        transfers.append(RemoteDMATransfer(dst_ids=[DstId(rid=rid, pnc=pid)], dma_engine_mask=1 << k,
                                           remote_sem=T.sem.arrived, src=src, dst=dst))
    g.remote_dma_fused(transfers, local_sem=T.sem.sent)
    return len(writes)


def rank_program(g, core, T, topo):
    rank = T.rank_of(core)
    sem = T.sem
    chip_base = core - core % 8

    if rank is None:
        if core % 8 != RELAY:
            return
        north, south, west, _east = _neighbours(T, T.rank_of(chip_base + 1))
        g.wait_ge(sem.arrived, 2)
        n = _send(g, T, topo, [
            (T.hop[FIRST], west, T.halo[EAST]),
            (T.hop[FIRST], north, T.halo[SOUTH]),
            (T.hop[LAST], south, T.halo[NORTH]),
        ])
        g.wait_ge(sem.sent, n)
        return

    north, south, west, east = _neighbours(T, rank)
    W = T.x.shape[1]

    g.sync.dma_start(T.edge[FIRST], T.x[:, 0:H]).then_inc(sem.loaded, 16)
    g.scalar.dma_start(T.edge[LAST], T.x[:, W - H:W]).then_inc(sem.loaded, 16)
    g.wait_ge(sem.loaded, 32)

    if topo.may_write(core, west) and topo.may_write(core, east):
        n = _send(g, T, topo, [
            (T.edge[LAST], east, T.halo[WEST]),
            (T.edge[FIRST], north, T.halo[SOUTH]),
            (T.edge[LAST], south, T.halo[NORTH]),
            (T.edge[FIRST], west, T.halo[EAST]),
        ])
    else:
        relay = chip_base + RELAY
        n = _send(g, T, topo, [
            (T.edge[FIRST], relay, T.hop[FIRST]),
            (T.edge[LAST], relay, T.hop[LAST]),
            (T.edge[LAST], east, T.halo[WEST]),
        ])

    g.sync.wait_ge(sem.arrived, 4)
    g.sync.dma_start(T.y[:], T.halo[:]).then_inc(sem.stored, 16)
    g.wait_ge(sem.sent, n)
    g.wait_ge(sem.stored, 16)
